import numpy as np
import ml_dtypes


def mxq(x, axis, fmt="e4m3"):
    dtype, down = {"e4m3": (ml_dtypes.float8_e4m3fn, 7), "e5m2": (ml_dtypes.float8_e5m2, 14)}[fmt]
    v = np.moveaxis(np.asarray(x, np.float32).astype(ml_dtypes.bfloat16).astype(np.float64), axis, -1)
    blocks = v.reshape(v.shape[:-1] + (-1, 32))
    amax = np.abs(blocks).max(-1, keepdims=True)
    byte = np.maximum(np.where(amax > 0, np.frexp(amax)[1] - 1 + 127, 0) - down, 1)
    scale = np.exp2(byte - 127.0)
    codes = (blocks / scale).astype(np.float32).astype(dtype).astype(np.float64)
    return np.moveaxis((codes * scale).reshape(v.shape), -1, axis)


WIDE = False


def mx_kscale(k):
    if not WIDE:
        return np.ones(k)
    levels = np.array([10, -10, 5, -5, 0])
    if k % 512:
        return np.exp2(np.random.permutation(np.resize(levels, k // 32))).repeat(32)
    a = np.empty((k // 512, 16))
    for p in range(k // 512):
        a[p, :8] = np.random.permutation(np.resize(levels, 8))
        for g in range(8):
            far = levels[np.abs(levels - a[p, g]) >= 10]
            a[p, g + 8] = far[np.random.randint(len(far))]
    return np.exp2(a.ravel()).repeat(32)


def f64(x):
    return np.asarray(x).astype(np.float64)


def striped(idx):
    return np.tile(idx.reshape(-1, 16).T, (8, 1)).astype(np.uint16)


def unstriped(offs):
    return offs[:16].T.reshape(-1).astype(np.int64)


E2M1 = np.array([0.0, 0.5, 1.0, 1.5, 2.0, 3.0, 4.0, 6.0, -0.0, -0.5, -1.0, -1.5, -2.0, -3.0, -4.0, -6.0])


def pack_weight(w, fmt):
    k, n = w.shape
    w = f64(np.asarray(w, np.float32).astype(ml_dtypes.bfloat16)).reshape(k // 32, 32, n)
    amax = np.abs(w).max(1)
    if fmt == "e4m3":
        byte = np.frexp(amax)[1] - 1 + 127 - 7
    else:
        mant, ex = np.frexp(amax / 6.0)
        byte = np.where(mant > 0.5, ex, ex - 1) + 127
    byte = np.clip(np.where(amax > 0, byte, 1), 1, 254)
    scaled = (w * np.exp2(127.0 - byte)[:, None, :]).reshape(k, n).astype(np.float32)
    by_word = np.ascontiguousarray(scaled.reshape(k // 512, 128, 4, n).transpose(0, 1, 3, 2))
    if fmt == "e4m3":
        words = by_word.astype(ml_dtypes.float8_e4m3fn).view(np.uint8)
    else:
        c = by_word.astype(ml_dtypes.float4_e2m1fn).view(np.uint8) & 0xF
        words = (c[..., 0::2] | (c[..., 1::2] << 4)).reshape(k // 512, 128, 2 * n)
    return np.ascontiguousarray(words), np.ascontiguousarray(byte.astype(np.uint8).reshape(k // 512, 16, n))


def unpack_weight(words, scales, fmt):
    g, _, n = scales.shape
    words = np.ascontiguousarray(words).reshape(g, 128, n, -1)
    if fmt == "e4m3":
        vals = words.view(ml_dtypes.float8_e4m3fn).astype(np.float64)
    else:
        nib = np.empty((g, 128, n, 4), np.uint8)
        nib[..., 0::2] = words & 0xF
        nib[..., 1::2] = words >> 4
        vals = E2M1[nib]
    vals = vals * np.repeat(np.exp2(scales.astype(np.float64) - 127.0), 8, axis=1)[..., None]
    return vals.transpose(0, 1, 3, 2).reshape(g * 512, n)


def gelu(v):
    return 0.5 * v * (1.0 + np.tanh(np.sqrt(2.0 / np.pi) * (v + 0.044715 * v**3)))


K, T, S, H, T2, P, N = 1536, 4096, 1024, 512, 2048, 1024, 768

def setup_inputs():
    n = np.random.standard_normal
    s = mx_kscale(K)[:, None]
    u = mx_kscale(H)[:, None]
    tab_words, tab_scales = pack_weight(n((K, T)) * s, "e4m3")
    w4_words, w4_scales = pack_weight(n((K, H)) / np.sqrt(K) / s, "e2m1")
    w8_words, w8_scales = pack_weight(2.0 * n((H, N)) / np.sqrt(H) / u, "e4m3")
    return {
        "tab_words": tab_words, "tab_scales": tab_scales,
        "offs": striped(np.random.permutation(T)[:S]),
        "w1": (1.5 * n((K, H)) / np.sqrt(K) / s).astype(np.float32),
        "w4_words": w4_words, "w4_scales": w4_scales,
        "page0": n((H, T2)).astype(np.float32),
        "wgs": np.exp(0.3 * n((128, S))).astype(np.float32),
        "offs2": striped(np.random.permutation(T2)[:S]),
        "offs3": striped(np.random.permutation(T2)[:P]),
        "bias": (0.5 * n(H)).astype(np.float32),
        "gain": (np.exp(0.3 * n(H)) * u[:, 0]).astype(np.float32),
        "w8_words": w8_words, "w8_scales": w8_scales,
    }

def reference(tab_words, tab_scales, offs, w1, w4_words, w4_scales, page0, wgs, offs2, offs3, bias, gain, w8_words, w8_scales):
    v = unpack_weight(tab_words, tab_scales, "e4m3")[:, unstriped(offs)]
    w4 = unpack_weight(w4_words, w4_scales, "e2m1")
    w8 = unpack_weight(w8_words, w8_scales, "e4m3")
    a = mxq(f64(w1), 0, "e4m3").T @ v
    b = w4.T @ v
    h = a / (1.0 + b * b)
    page = f64(page0).copy()
    page[:, unstriped(offs2)] = np.tile(f64(wgs), (H // 128, 1)) * h
    x = page[:, unstriped(offs3)]
    z = f64(gain)[:, None] / (1.0 + np.exp(-(x + f64(bias)[:, None])))
    return w8.T @ mxq(z, 0, "e4m3")

@@ -1,0 +1,307 @@
+from contextlib import ExitStack
+
+import concourse.mybir as mybir
+from concourse.masks import make_identity
+
+K, T, S, H, T2, M, N = 1536, 4096, 1024, 512, 2048, 1024, 768
+FLOPS = 2 * 2 * K * H * S + 2 * H * N * M
+
+F32 = mybir.dt.float32
+BF16 = mybir.dt.bfloat16
+I32 = mybir.dt.int32
+U32 = mybir.dt.uint32
+U16 = mybir.dt.uint16
+U8 = mybir.dt.uint8
+FP8X4 = mybir.dt.float8_e4m3fn_x4
+FP4X4 = mybir.dt.float4_e2m1fn_x4
+ACT = mybir.ActivationFunctionType
+MULT = mybir.AluOpType.mult
+
+P = 128
+PACK = 4
+PASSES = K // (P * PACK)
+QUADS = 4
+BANK = 512
+HALVES = S // BANK
+MQ = 256
+LIST_ROW = 16
+
+
+def tile_list_coupon_redemption_ratios_kernel(
+    tc, tab_words, tab_scales, offs, w1, w4_words, w4_scales, page0, wgs, offs2, offs3, bias, gain, w8_words, w8_scales, out
+):
+    nc = tc.nc
+    with ExitStack() as ctx:
+        keep = ctx.enter_context(tc.tile_pool(name="keep", bufs=1))
+        ring = ctx.enter_context(tc.tile_pool(name="ring", bufs=2))
+        psum = ctx.enter_context(tc.psum_pool(name="psum", bufs=4))
+
+        def held(name, shape, dtype):
+            return keep.tile(shape, dtype, name=name, align_bytes=64)
+
+        def cols(h, width=BANK):
+            return slice(h * width, (h + 1) * width)
+
+        def entries(h, width=BANK):
+            return slice(h * width // LIST_ROW, (h + 1) * width // LIST_ROW)
+
+        idx = held("idx", [P, S // LIST_ROW], U16)
+        idx2 = held("idx2", [P, S // LIST_ROW], U16)
+        idx3 = held("idx3", [P, M // LIST_ROW], U16)
+        tab = [held("tab%d" % a, [P, T], I32) for a in range(PASSES)]
+        tab_sc = held("tab_sc", [P, T], U8)
+        picked = [held("picked%d" % a, [P, S], U32) for a in range(PASSES)]
+        picked_sc_rows = held("picked_sc_rows", [P, S], U8)
+        picked_sc = held("picked_sc", [P, PASSES * S], U8)
+        w4_raw = held("w4_raw", [P, PASSES * H * 2], U8)
+        w4 = held("w4", [P, PASSES * H * 2], U8)
+        w4_sc_raw = held("w4_sc_raw", [P, PASSES * H], U8)
+        w4_sc = held("w4_sc", [P, PASSES * H], U8)
+        w1_codes = [held("w1_codes%d" % a, [P, H], U32) for a in range(PASSES)]
+        w1_sc = [held("w1_sc%d" % a, [P, H], U8) for a in range(PASSES)]
+        w8 = held("w8", [P, N], I32)
+        w8_sc = held("w8_sc", [P, N], U8)
+        page = [held("page%d" % t, [P, T2], F32) for t in range(PACK)]
+        wgs_rows = held("wgs_rows", [P, S], F32)
+        weight = [held("weight%d" % t, [P, S], F32) for t in range(PACK)]
+        damp = [held("damp%d" % t, [P, S], F32) for t in range(PACK)]
+        bias_sb = held("bias_sb", [P, PACK], F32)
+        gain_sb = held("gain_sb", [P, PACK], F32)
+        z = [held("z%d" % u, [P, MQ, PACK], BF16) for u in range(M // MQ)]
+        z_codes = [held("z_codes%d" % u, [P, MQ], U32) for u in range(M // MQ)]
+        z_sc = [held("z_sc%d" % u, [P, MQ], U8) for u in range(M // MQ)]
+        ident = held("ident", [P, P], F32)
+        warm = held("warm", [P, 2], F32)
+
+        nc.vector.memset(tab_sc[:].bitcast(I32), 0)
+        nc.vector.memset(warm[:, 0:1], 1.0)
+        nc.scalar.activation(warm[:, 1:2], warm[:, 0:1], ACT.Abs_reciprocal_sqrt)
+        nc.vector.memset(w4_sc_raw[:].bitcast(I32), 0)
+        nc.vector.memset(picked_sc[:].bitcast(I32), 0)
+        nc.vector.memset(w8_sc[:].bitcast(I32), 0)
+        make_identity(nc, ident[:])
+
+        def load_tab(a):
+            nc.sync.dma_start(tab[a][:], tab_words[a].rearrange("p t i -> p (t i)").bitcast(I32))
+
+        w1_raw = {}
+
+        def load_w1(a):
+            w1_raw[a] = ring.tile([P, PACK, H], F32, name="w1_raw", tag="wide", bufs=3, align_bytes=64)
+            nc.sync.dma_start(w1_raw[a][:], w1[a * P * PACK : (a + 1) * P * PACK, :].rearrange("(p j) r -> p j r", j=PACK))
+
+        def load_page(t):
+            nc.sync.dma_start(page[t][:], page0.rearrange("(p t) c -> p t c", t=PACK)[:, t, :])
+
+        load_w1(0)
+        nc.sync.dma_start(
+            tab_sc[0 : PASSES * 16, :].bitcast(I32), tab_scales.bitcast(I32).rearrange("a q t -> q a t")
+        )
+        nc.sync.dma_start(idx[:], offs)
+        nc.sync.dma_start(wgs_rows[:], wgs)
+        nc.sync.dma_start(
+            w4_raw[:].bitcast(I32).rearrange("p (a c) -> p a c", a=PASSES), w4_words.bitcast(I32).rearrange("a p c -> p a c")
+        )
+        load_tab(0)
+        for q in range(QUADS):
+            nc.sync.dma_start(
+                w4_sc_raw[32 * q : 32 * q + 4, :].bitcast(I32).rearrange("p (a c) -> p a c", a=PASSES),
+                w4_scales.bitcast(I32)[:, 4 * q : 4 * q + 4, :].rearrange("a r c -> r a c"),
+            )
+        load_w1(1)
+        load_tab(1)
+        load_tab(2)
+        load_w1(2)
+        nc.sync.dma_start(idx2[:], offs2)
+        load_page(0)
+        nc.sync.dma_start(idx3[:], offs3)
+        load_page(1)
+        nc.sync.dma_start(bias_sb[:], bias.rearrange("(p t) -> p t", t=PACK))
+        nc.sync.dma_start(gain_sb[:], gain.rearrange("(p t) -> p t", t=PACK))
+        load_page(2)
+        load_page(3)
+        nc.sync.dma_start(w8[:], w8_words[0].rearrange("p c i -> p (c i)").bitcast(I32))
+        for q in range(QUADS):
+            nc.sync.dma_start(w8_sc[32 * q : 32 * q + 4, :].bitcast(I32), w8_scales.bitcast(I32)[0, 4 * q : 4 * q + 4, :])
+
+        def gather_words(a, picks, where):
+            nc.vector.tensor_copy(picked[a][:, where], tab[a][:].bitcast(U32).indirect(picks))
+
+        def quantize_w1(a, t0, t1, cast):
+            grouped = ring.tile([P, (t1 - t0) * P * PACK], BF16, name="w1_grouped", align_bytes=64)
+            cast(
+                grouped[:].rearrange("p (t m j) -> p m t j", t=t1 - t0, j=PACK),
+                w1_raw[a][:].rearrange("p j (m t) -> p m t j", t=PACK)[:, :, t0:t1, :],
+            )
+            where = slice(t0 * P, t1 * P)
+            nc.vector.quantize_mx(out=w1_codes[a][:, where].bitcast(FP8X4), scales=w1_sc[a][:, where], in_=grouped[:])
+
+        quantize_w1(0, 0, PACK, nc.vector.tensor_copy)
+        nc.vector.tensor_copy(picked_sc_rows[:], tab_sc[:].indirect(idx[:]))
+        for q in range(QUADS):
+            nc.scalar.dma_start(
+                picked_sc[32 * q : 32 * q + 4, :].bitcast(I32).rearrange("p (a c) -> p a c", a=PASSES),
+                picked_sc_rows[12 * q : 12 * q + 12, :].bitcast(I32),
+            )
+        nc.vector.tensor_copy(
+            w4[:].bitcast(U16).rearrange("p (a t m) -> p a t m", a=PASSES, t=PACK),
+            w4_raw[:].bitcast(U16).rearrange("p (a m t) -> p a t m", a=PASSES, t=PACK),
+        )
+        nc.vector.tensor_copy(
+            w4_sc[:].rearrange("p (a t m) -> p a t m", a=PASSES, t=PACK),
+            w4_sc_raw[:].rearrange("p (a m t) -> p a t m", a=PASSES, t=PACK),
+        )
+
+        for h in range(HALVES):
+            turned = psum.tile([P, PACK, P], F32, name="turned", tag="bank_b")
+            for i in range(PACK):
+                nc.tensor.transpose(turned[:, i, :], wgs_rows[:, cols(h * PACK + i, P)], ident[:])
+            spread = ring.tile([P, PACK, PACK, QUADS, 32], F32, name="spread")
+            for i in range(PACK):
+                nc.scalar.copy(
+                    spread[:, i],
+                    turned[:, i, :].rearrange("j (q t) -> j t q", t=PACK).unsqueeze(2).to_broadcast([P, PACK, QUADS, 32]),
+                )
+            for t in range(PACK):
+                back = psum.tile([P, PACK, P], F32, name="back", tag="bank_a")
+                for i in range(PACK):
+                    nc.tensor.transpose(back[:, i, :], spread[:, i, t].rearrange("j u q -> j (u q)"), ident[:])
+                nc.scalar.copy(weight[t][:, cols(h)], back[:].rearrange("p i j -> p (i j)"))
+
+        def exposure_pass(acc, a, t, h):
+            c0 = a * H + t * P
+            nc.tensor.matmul_mx(
+                out=acc[:],
+                lhsT=w4[:, 2 * c0 : 2 * (c0 + P)].bitcast(FP4X4),
+                lhsT_scale=w4_sc[:, c0 : c0 + P],
+                rhs=picked[a][:, cols(h)].bitcast(FP8X4),
+                rhs_scale=picked_sc[:, a * S + h * BANK : a * S + (h + 1) * BANK],
+                start=(a == 0),
+                stop=(a == PASSES - 1),
+            )
+
+        def signal_pass(acc, a, t, h):
+            nc.tensor.matmul_mx(
+                out=acc[:],
+                lhsT=w1_codes[a][:, cols(t, P)].bitcast(FP8X4),
+                lhsT_scale=w1_sc[a][:, cols(t, P)],
+                rhs=picked[a][:, cols(h)].bitcast(FP8X4),
+                rhs_scale=picked_sc[:, a * S + h * BANK : a * S + (h + 1) * BANK],
+                start=(a == 0),
+                stop=(a == PASSES - 1),
+            )
+
+        def damping(acc, t, h, lo=0, hi=BANK):
+            part = damp[t][:, h * BANK + lo : h * BANK + hi]
+            nc.scalar.activation(part, acc[:, lo:hi], ACT.Square)
+            nc.scalar.activation(part, part, ACT.Abs_reciprocal_sqrt, bias=1.0)
+            nc.scalar.activation(part, part, ACT.Square)
+
+        first = [(t, h) for t in range(2) for h in range(HALVES)]
+        later = [(t, h) for t in range(2, PACK) for h in range(HALVES)]
+        exposure = {th: psum.tile([P, BANK], F32, name="exposure", tag="bank_b") for th in first}
+        signal = {th: psum.tile([P, BANK], F32, name="signal", tag="bank_a") for th in first}
+
+        gather_words(0, idx[:], slice(0, S))
+        quantize_w1(1, 0, PACK, nc.vector.tensor_copy)
+        gather_words(1, idx[:], slice(0, S))
+        for a in range(PASSES - 1):
+            for t, h in first:
+                exposure_pass(exposure[t, h], a, t, h)
+                signal_pass(signal[t, h], a, t, h)
+        last = PASSES - 1
+        for h in range(HALVES):
+            gather_words(last, idx[:, entries(h)], cols(h))
+        for t, h in first:
+            exposure_pass(exposure[t, h], last, t, h)
+        quantize_w1(last, 0, 2, nc.vector.tensor_copy)
+        for t, h in first:
+            signal_pass(signal[t, h], last, t, h)
+        for lo in range(0, BANK, MQ):
+            damping(exposure[0, 0], 0, 0, lo, lo + MQ)
+        for t, h in first[1:]:
+            damping(exposure[t, h], t, h)
+        quantize_w1(last, 2, PACK, nc.scalar.copy)
+        for t, h in later:
+            exposure[t, h] = psum.tile([P, BANK], F32, name="exposure", tag="bank_b")
+            for a in range(PASSES):
+                exposure_pass(exposure[t, h], a, t, h)
+            damping(exposure[t, h], t, h)
+
+        ratio = {}
+
+        def make_ratio(t, lo, hi):
+            h = lo // BANK
+            if lo == 0:
+                ratio[t] = ring.tile([P, S], F32, name="ratio")
+            nc.vector.tensor_tensor(ratio[t][:, lo:hi], signal[t, h][:, lo - h * BANK : hi - h * BANK], damp[t][:, lo:hi], MULT)
+
+        def next_signal(t):
+            for h in range(HALVES):
+                signal[t, h] = psum.tile([P, BANK], F32, name="signal", tag="bank_a")
+                for a in range(PASSES):
+                    signal_pass(signal[t, h], a, t, h)
+
+        def put(t, lo, hi):
+            nc.vector.tensor_tensor(
+                page[t][:].indirect(idx2[:, lo // LIST_ROW : hi // LIST_ROW]), ratio[t][:, lo:hi], weight[t][:, lo:hi], MULT
+            )
+
+        def fetch(t, fetched, part, width):
+            where = cols(part, width)
+            nc.vector.tensor_copy(fetched[:, where], page[t][:].indirect(idx3[:, entries(part, width)]))
+            nc.scalar.activation(fetched[:, where], fetched[:, where], ACT.Sigmoid, bias=bias_sb[:, t : t + 1])
+            for u in range(part * width // MQ, (part + 1) * width // MQ):
+                nc.scalar.activation(z[u][:, :, t], fetched[:, cols(u, MQ)], ACT.Copy, scale=gain_sb[:, t : t + 1])
+
+        def quantize_z(part):
+            nc.vector.quantize_mx(
+                out=z_codes[part][:].bitcast(FP8X4), scales=z_sc[part][:], in_=z[part][:].rearrange("p m t -> p (m t)")
+            )
+
+        for t in range(PACK):
+            if t == 0:
+                pieces = [(0, MQ), (MQ, BANK), (BANK, S)]
+                make_ratio(t, *pieces[0])
+                for i, piece in enumerate(pieces):
+                    if i + 1 < len(pieces):
+                        make_ratio(t, *pieces[i + 1])
+                    put(t, *piece)
+            else:
+                put(t, 0, S)
+            if t + 2 < PACK:
+                next_signal(t + 2)
+            fetched = ring.tile([P, M], F32, name="fetched")
+            if t + 1 < PACK:
+                for h in range(HALVES):
+                    make_ratio(t + 1, h * BANK, (h + 1) * BANK)
+                fetch(t, fetched, 0, M)
+            else:
+                for part in range(M // MQ):
+                    fetch(t, fetched, part, MQ)
+                    quantize_z(part)
+
+        out_rows = out.rearrange("(c p) m -> p c m", p=P)
+        pair = BANK // MQ
+        for part in range(M // MQ):
+            where = cols(part, MQ)
+            staged = ring.tile([P, N // P, MQ], F32, name="staged", tag="wide", bufs=3, align_bytes=64)
+            for i in range(N // P // pair):
+                scores = psum.tile([P, pair, MQ], F32, name="scores", tag="bank_b" if i % 2 else "bank_a")
+                for c in range(pair):
+                    n_cols = cols(i * pair + c, P)
+                    nc.tensor.matmul_mx(
+                        out=scores[:, c, :],
+                        lhsT=w8[:, n_cols].bitcast(FP8X4),
+                        lhsT_scale=w8_sc[:, n_cols],
+                        rhs=z_codes[part][:].bitcast(FP8X4),
+                        rhs_scale=z_sc[part][:],
+                        start=True,
+                        stop=True,
+                    )
+                rows = slice(i * pair, (i + 1) * pair)
+                if i % 2:
+                    nc.scalar.copy(staged[:, rows, :], scores[:])
+                else:
+                    nc.vector.tensor_copy(staged[:, rows, :], scores[:])
+                nc.sync.dma_start(out_rows[:, rows, where], staged[:, rows, :])

@@ -25,6 +25,7 @@ BANK = 512
 HALVES = S // BANK
 MQ = 256
 LIST_ROW = 16
+EARLY = 2
 
 
 def tile_list_coupon_redemption_ratios_kernel(
@@ -67,7 +68,7 @@ def tile_list_coupon_redemption_ratios_kernel(
         damp = [held("damp%d" % t, [P, S], F32) for t in range(PACK)]
         bias_sb = held("bias_sb", [P, PACK], F32)
         gain_sb = held("gain_sb", [P, PACK], F32)
-        z = [held("z%d" % u, [P, MQ, PACK], BF16) for u in range(M // MQ)]
+        z = [keep.tile([P, MQ, PACK], BF16, name="z", tag="z", bufs=M // MQ, align_bytes=64) for u in range(M // MQ)]
         z_codes = [held("z_codes%d" % u, [P, MQ], U32) for u in range(M // MQ)]
         z_sc = [held("z_sc%d" % u, [P, MQ], U8) for u in range(M // MQ)]
         ident = held("ident", [P, P], F32)
@@ -191,11 +192,16 @@ def tile_list_coupon_redemption_ratios_kernel(
                 stop=(a == PASSES - 1),
             )
 
+        scratch = {}
+
         def damping(acc, t, h, lo=0, hi=BANK):
-            part = damp[t][:, h * BANK + lo : h * BANK + hi]
+            if h == 0 and lo == 0:
+                scratch[t] = keep.tile([P, S], F32, name="scratch")
+            where = slice(h * BANK + lo, h * BANK + hi)
+            part = scratch[t][:, where]
             nc.scalar.activation(part, acc[:, lo:hi], ACT.Square)
             nc.scalar.activation(part, part, ACT.Abs_reciprocal_sqrt, bias=1.0)
-            nc.scalar.activation(part, part, ACT.Square)
+            nc.scalar.activation(damp[t][:, where], part, ACT.Square)
 
         first = [(t, h) for t in range(2) for h in range(HALVES)]
         later = [(t, h) for t in range(2, PACK) for h in range(HALVES)]
@@ -247,12 +253,16 @@ def tile_list_coupon_redemption_ratios_kernel(
                 page[t][:].indirect(idx2[:, lo // LIST_ROW : hi // LIST_ROW]), ratio[t][:, lo:hi], weight[t][:, lo:hi], MULT
             )
 
-        def fetch(t, fetched, part, width):
-            where = cols(part, width)
-            nc.vector.tensor_copy(fetched[:, where], page[t][:].indirect(idx3[:, entries(part, width)]))
-            nc.scalar.activation(fetched[:, where], fetched[:, where], ACT.Sigmoid, bias=bias_sb[:, t : t + 1])
-            for u in range(part * width // MQ, (part + 1) * width // MQ):
-                nc.scalar.activation(z[u][:, :, t], fetched[:, cols(u, MQ)], ACT.Copy, scale=gain_sb[:, t : t + 1])
+        def fetch(t, first_part, parts, fetched, gate, on_vector):
+            lo, hi = first_part * MQ, (first_part + parts) * MQ
+            nc.vector.tensor_copy(fetched, page[t][:].indirect(idx3[:, lo // LIST_ROW : hi // LIST_ROW]))
+            nc.scalar.activation(gate, fetched, ACT.Sigmoid, bias=bias_sb[:, t : t + 1])
+            for u in range(parts):
+                slot = z[first_part + u][:, :, t]
+                if on_vector:
+                    nc.vector.tensor_scalar(slot, gate[:, cols(u, MQ)], gain_sb[:, t : t + 1], None, MULT)
+                else:
+                    nc.scalar.activation(slot, gate[:, cols(u, MQ)], ACT.Copy, scale=gain_sb[:, t : t + 1])
 
         def quantize_z(part):
             nc.vector.quantize_mx(
@@ -271,14 +281,20 @@ def tile_list_coupon_redemption_ratios_kernel(
                 put(t, 0, S)
             if t + 2 < PACK:
                 next_signal(t + 2)
-            fetched = ring.tile([P, M], F32, name="fetched")
+            gate = keep.tile([P, S], F32, name="scratch")
             if t + 1 < PACK:
                 for h in range(HALVES):
                     make_ratio(t + 1, h * BANK, (h + 1) * BANK)
-                fetch(t, fetched, 0, M)
+                parts = EARLY if t + 2 == PACK else M // MQ
+                fetch(t, 0, parts, damp[t + 1][:, : parts * MQ], gate[:, : parts * MQ], False)
             else:
-                for part in range(M // MQ):
-                    fetch(t, fetched, part, MQ)
+                for part in range(EARLY):
+                    fetch(t, part, 1, damp[0][:, cols(part, MQ)], gate[:, cols(part, MQ)], True)
+                    quantize_z(part)
+                for part in range(EARLY, M // MQ):
+                    late = keep.tile([P, 2, MQ], F32, name="late", tag="z", bufs=M // MQ, align_bytes=64)
+                    for i in range(2):
+                        fetch(t - 1 + i, part, 1, late[:, i, :], late[:, i, :], True)
                     quantize_z(part)
 
         out_rows = out.rearrange("(c p) m -> p c m", p=P)
@@ -286,10 +302,11 @@ def tile_list_coupon_redemption_ratios_kernel(
         for part in range(M // MQ):
             where = cols(part, MQ)
             staged = ring.tile([P, N // P, MQ], F32, name="staged", tag="wide", bufs=3, align_bytes=64)
-            for i in range(N // P // pair):
-                scores = psum.tile([P, pair, MQ], F32, name="scores", tag="bank_b" if i % 2 else "bank_a")
-                for c in range(pair):
-                    n_cols = cols(i * pair + c, P)
+            per_bank = 1 if part + 1 == M // MQ else pair
+            for i in range(N // P // per_bank):
+                scores = psum.tile([P, per_bank, MQ], F32, name="scores", tag="bank_b" if i % 2 else "bank_a")
+                for c in range(per_bank):
+                    n_cols = cols(i * per_bank + c, P)
                     nc.tensor.matmul_mx(
                         out=scores[:, c, :],
                         lhsT=w8[:, n_cols].bitcast(FP8X4),
@@ -299,9 +316,11 @@ def tile_list_coupon_redemption_ratios_kernel(
                         start=True,
                         stop=True,
                     )
-                rows = slice(i * pair, (i + 1) * pair)
-                if i % 2:
+                rows = slice(i * per_bank, (i + 1) * per_bank)
+                if part < EARLY or (i + part) % 2:
                     nc.scalar.copy(staged[:, rows, :], scores[:])
                 else:
                     nc.vector.tensor_copy(staged[:, rows, :], scores[:])
-                nc.sync.dma_start(out_rows[:, rows, where], staged[:, rows, :])
+                if rows.stop % pair == 0:
+                    both = slice(rows.stop - pair, rows.stop)
+                    nc.sync.dma_start(out_rows[:, both, where], staged[:, both, :])

@@ -96,7 +96,7 @@ def tile_list_coupon_redemption_ratios_kernel(
 
         load_w1(0)
         nc.sync.dma_start(
-            tab_sc[0 : PASSES * 16, :].bitcast(I32), tab_scales.bitcast(I32).rearrange("a q t -> q a t")
+            tab_sc[0 : 2 * PASSES * 16 : 2, :].bitcast(I32), tab_scales.bitcast(I32).rearrange("a q t -> q a t")
         )
         nc.sync.dma_start(idx[:], offs)
         nc.sync.dma_start(wgs_rows[:], wgs)
@@ -142,7 +142,7 @@ def tile_list_coupon_redemption_ratios_kernel(
         for q in range(QUADS):
             nc.scalar.dma_start(
                 picked_sc[32 * q : 32 * q + 4, :].bitcast(I32).rearrange("p (a c) -> p a c", a=PASSES),
-                picked_sc_rows[12 * q : 12 * q + 12, :].bitcast(I32),
+                picked_sc_rows[24 * q : 24 * q + 24 : 2, :].bitcast(I32),
             )
         nc.vector.tensor_copy(
             w4[:].bitcast(U16).rearrange("p (a t m) -> p a t m", a=PASSES, t=PACK),
@@ -221,37 +221,43 @@ def tile_list_coupon_redemption_ratios_kernel(
         for t, h in first:
             exposure_pass(exposure[t, h], last, t, h)
         quantize_w1(last, 0, 2, nc.vector.tensor_copy)
+        quantize_w1(last, 2, PACK, nc.vector.tensor_copy)
         for t, h in first:
             signal_pass(signal[t, h], last, t, h)
+        entry = {}
+
+        def places(t, lo, hi):
+            return page[t][:].indirect(idx2[:, lo // LIST_ROW : hi // LIST_ROW])
+
         for lo in range(0, BANK, MQ):
             damping(exposure[0, 0], 0, 0, lo, lo + MQ)
-        for t, h in first[1:]:
-            damping(exposure[t, h], t, h)
-        quantize_w1(last, 2, PACK, nc.scalar.copy)
-        for t, h in later:
-            exposure[t, h] = psum.tile([P, BANK], F32, name="exposure", tag="bank_b")
-            for a in range(PASSES):
-                exposure_pass(exposure[t, h], a, t, h)
-            damping(exposure[t, h], t, h)
+        damping(exposure[0, 1], 0, 1)
 
-        ratio = {}
+        entry[0] = ring.tile([P, S], F32, name="entry", bufs=3)
+        for lo in range(0, BANK, MQ):
+            nc.vector.tensor_tensor(entry[0][:, lo : lo + MQ], signal[0, 0][:, lo : lo + MQ], damp[0][:, lo : lo + MQ], MULT)
+        nc.vector.tensor_tensor(places(0, 0, MQ), entry[0][:, :MQ], weight[0][:, :MQ], MULT)
+        nc.vector.tensor_tensor(entry[0][:, BANK:], signal[0, 1][:], damp[0][:, BANK:], MULT)
+        second = damp[0][:, BANK : BANK + MQ]
+        nc.vector.tensor_tensor(second, entry[0][:, MQ:BANK], weight[0][:, MQ:BANK], MULT)
+        nc.vector.tensor_copy(places(0, MQ, BANK), second)
+        nc.gpsimd.tensor_tensor(entry[0][:, BANK:], entry[0][:, BANK:], weight[0][:, BANK:], MULT)
+        nc.vector.tensor_copy(places(0, BANK, S), entry[0][:, BANK:])
 
-        def make_ratio(t, lo, hi):
-            h = lo // BANK
-            if lo == 0:
-                ratio[t] = ring.tile([P, S], F32, name="ratio")
-            nc.vector.tensor_tensor(ratio[t][:, lo:hi], signal[t, h][:, lo - h * BANK : hi - h * BANK], damp[t][:, lo:hi], MULT)
-
-        def next_signal(t):
+        for t in range(1, PACK):
+            entry[t] = ring.tile([P, S], F32, name="entry", bufs=3)
             for h in range(HALVES):
-                signal[t, h] = psum.tile([P, BANK], F32, name="signal", tag="bank_a")
-                for a in range(PASSES):
-                    signal_pass(signal[t, h], a, t, h)
-
-        def put(t, lo, hi):
-            nc.vector.tensor_tensor(
-                page[t][:].indirect(idx2[:, lo // LIST_ROW : hi // LIST_ROW]), ratio[t][:, lo:hi], weight[t][:, lo:hi], MULT
-            )
+                if (t, h) in later:
+                    exposure[t, h] = psum.tile([P, BANK], F32, name="exposure", tag="bank_b")
+                    signal[t, h] = psum.tile([P, BANK], F32, name="signal", tag="bank_a")
+                    for a in range(PASSES):
+                        exposure_pass(exposure[t, h], a, t, h)
+                    for a in range(PASSES):
+                        signal_pass(signal[t, h], a, t, h)
+                damping(exposure[t, h], t, h)
+                nc.scalar.copy(entry[t][:, cols(h)], signal[t, h][:])
+                nc.gpsimd.tensor_tensor(damp[t][:, cols(h)], damp[t][:, cols(h)], weight[t][:, cols(h)], MULT)
+                nc.gpsimd.tensor_tensor(entry[t][:, cols(h)], entry[t][:, cols(h)], damp[t][:, cols(h)], MULT)
 
         def fetch(t, first_part, parts, fetched, gate, on_vector):
             lo, hi = first_part * MQ, (first_part + parts) * MQ
@@ -270,23 +276,12 @@ def tile_list_coupon_redemption_ratios_kernel(
             )
 
         for t in range(PACK):
-            if t == 0:
-                pieces = [(0, MQ), (MQ, BANK), (BANK, S)]
-                make_ratio(t, *pieces[0])
-                for i, piece in enumerate(pieces):
-                    if i + 1 < len(pieces):
-                        make_ratio(t, *pieces[i + 1])
-                    put(t, *piece)
-            else:
-                put(t, 0, S)
-            if t + 2 < PACK:
-                next_signal(t + 2)
+            if t > 0:
+                nc.vector.tensor_copy(places(t, 0, S), entry[t][:])
             gate = keep.tile([P, S], F32, name="scratch")
             if t + 1 < PACK:
-                for h in range(HALVES):
-                    make_ratio(t + 1, h * BANK, (h + 1) * BANK)
                 parts = EARLY if t + 2 == PACK else M // MQ
-                fetch(t, 0, parts, damp[t + 1][:, : parts * MQ], gate[:, : parts * MQ], False)
+                fetch(t, 0, parts, weight[t][:, : parts * MQ], gate[:, : parts * MQ], False)
             else:
                 for part in range(EARLY):
                     fetch(t, part, 1, damp[0][:, cols(part, MQ)], gate[:, cols(part, MQ)], True)
@@ -302,7 +297,8 @@ def tile_list_coupon_redemption_ratios_kernel(
         for part in range(M // MQ):
             where = cols(part, MQ)
             staged = ring.tile([P, N // P, MQ], F32, name="staged", tag="wide", bufs=3, align_bytes=64)
-            per_bank = 1 if part + 1 == M // MQ else pair
+            per_bank = 1 if part in (0, M // MQ - 1) else pair
+            per_store = 1 if part == 0 else pair
             for i in range(N // P // per_bank):
                 scores = psum.tile([P, per_bank, MQ], F32, name="scores", tag="bank_b" if i % 2 else "bank_a")
                 for c in range(per_bank):
@@ -321,6 +317,6 @@ def tile_list_coupon_redemption_ratios_kernel(
                     nc.scalar.copy(staged[:, rows, :], scores[:])
                 else:
                     nc.vector.tensor_copy(staged[:, rows, :], scores[:])
-                if rows.stop % pair == 0:
-                    both = slice(rows.stop - pair, rows.stop)
+                if rows.stop % per_store == 0:
+                    both = slice(rows.stop - per_store, rows.stop)
                     nc.sync.dma_start(out_rows[:, both, where], staged[:, both, :])

@@ -16,6 +16,7 @@ FP8X4 = mybir.dt.float8_e4m3fn_x4
 FP4X4 = mybir.dt.float4_e2m1fn_x4
 ACT = mybir.ActivationFunctionType
 MULT = mybir.AluOpType.mult
+ADD = mybir.AluOpType.add
 
 P = 128
 PACK = 4
@@ -25,6 +26,7 @@ BANK = 512
 HALVES = S // BANK
 MQ = 256
 LIST_ROW = 16
+BANKS = 8
 EARLY = 2
 
 
@@ -35,10 +37,13 @@ def tile_list_coupon_redemption_ratios_kernel(
     with ExitStack() as ctx:
         keep = ctx.enter_context(tc.tile_pool(name="keep", bufs=1))
         ring = ctx.enter_context(tc.tile_pool(name="ring", bufs=2))
-        psum = ctx.enter_context(tc.psum_pool(name="psum", bufs=4))
+        psum = ctx.enter_context(tc.psum_pool(name="psum", bufs=1))
 
         def held(name, shape, dtype):
             return keep.tile(shape, dtype, name=name, align_bytes=64)
+
+        def bank(number, shape):
+            return psum.tile(shape, F32, name="bank", tag="bank%d" % number)
 
         def cols(h, width=BANK):
             return slice(h * width, (h + 1) * width)
@@ -154,7 +159,7 @@ def tile_list_coupon_redemption_ratios_kernel(
         )
 
         for h in range(HALVES):
-            turned = psum.tile([P, PACK, P], F32, name="turned", tag="bank_b")
+            turned = bank(h, [P, PACK, P])
             for i in range(PACK):
                 nc.tensor.transpose(turned[:, i, :], wgs_rows[:, cols(h * PACK + i, P)], ident[:])
             spread = ring.tile([P, PACK, PACK, QUADS, 32], F32, name="spread")
@@ -164,7 +169,7 @@ def tile_list_coupon_redemption_ratios_kernel(
                     turned[:, i, :].rearrange("j (q t) -> j t q", t=PACK).unsqueeze(2).to_broadcast([P, PACK, QUADS, 32]),
                 )
             for t in range(PACK):
-                back = psum.tile([P, PACK, P], F32, name="back", tag="bank_a")
+                back = bank(PACK + t, [P, PACK, P])
                 for i in range(PACK):
                     nc.tensor.transpose(back[:, i, :], spread[:, i, t].rearrange("j u q -> j (u q)"), ident[:])
                 nc.scalar.copy(weight[t][:, cols(h)], back[:].rearrange("p i j -> p (i j)"))
@@ -203,72 +208,77 @@ def tile_list_coupon_redemption_ratios_kernel(
             nc.scalar.activation(part, part, ACT.Abs_reciprocal_sqrt, bias=1.0)
             nc.scalar.activation(damp[t][:, where], part, ACT.Square)
 
-        first = [(t, h) for t in range(2) for h in range(HALVES)]
-        later = [(t, h) for t in range(2, PACK) for h in range(HALVES)]
-        exposure = {th: psum.tile([P, BANK], F32, name="exposure", tag="bank_b") for th in first}
-        signal = {th: psum.tile([P, BANK], F32, name="signal", tag="bank_a") for th in first}
+        blocks = [(t, h) for t in range(PACK) for h in range(HALVES)]
+        opened = blocks[: 2 * HALVES]
+        exposure = {(t, h): bank(HALVES * t + h, [P, BANK]) for t, h in opened}
+        signal = {(0, h): bank(2 * HALVES + h, [P, BANK]) for h in range(HALVES)}
 
         gather_words(0, idx[:], slice(0, S))
         quantize_w1(1, 0, PACK, nc.vector.tensor_copy)
         gather_words(1, idx[:], slice(0, S))
-        for a in range(PASSES - 1):
-            for t, h in first:
-                exposure_pass(exposure[t, h], a, t, h)
-                signal_pass(signal[t, h], a, t, h)
         last = PASSES - 1
+        for a in range(last):
+            for t, h in opened:
+                exposure_pass(exposure[t, h], a, t, h)
+            for h in range(HALVES):
+                signal_pass(signal[0, h], a, 0, h)
         for h in range(HALVES):
             gather_words(last, idx[:, entries(h)], cols(h))
-        for t, h in first:
-            exposure_pass(exposure[t, h], last, t, h)
+        for h in range(HALVES):
+            exposure_pass(exposure[0, h], last, 0, h)
         quantize_w1(last, 0, 2, nc.vector.tensor_copy)
         quantize_w1(last, 2, PACK, nc.vector.tensor_copy)
-        for t, h in first:
-            signal_pass(signal[t, h], last, t, h)
+        for h in range(HALVES):
+            signal_pass(signal[0, h], last, 0, h)
+        for t, h in opened[HALVES:]:
+            exposure_pass(exposure[t, h], last, t, h)
+
         entry = {}
 
-        def places(t, lo, hi):
-            return page[t][:].indirect(idx2[:, lo // LIST_ROW : hi // LIST_ROW])
-
-        for lo in range(0, BANK, MQ):
-            damping(exposure[0, 0], 0, 0, lo, lo + MQ)
-        damping(exposure[0, 1], 0, 1)
+        def put(t, lo, hi):
+            nc.vector.tensor_copy(page[t][:].indirect(idx2[:, lo // LIST_ROW : hi // LIST_ROW]), entry[t][:, lo:hi])
 
         entry[0] = ring.tile([P, S], F32, name="entry", bufs=3)
-        for lo in range(0, BANK, MQ):
-            nc.vector.tensor_tensor(entry[0][:, lo : lo + MQ], signal[0, 0][:, lo : lo + MQ], damp[0][:, lo : lo + MQ], MULT)
-        nc.vector.tensor_tensor(places(0, 0, MQ), entry[0][:, :MQ], weight[0][:, :MQ], MULT)
-        nc.vector.tensor_tensor(entry[0][:, BANK:], signal[0, 1][:], damp[0][:, BANK:], MULT)
-        second = damp[0][:, BANK : BANK + MQ]
-        nc.vector.tensor_tensor(second, entry[0][:, MQ:BANK], weight[0][:, MQ:BANK], MULT)
-        nc.vector.tensor_copy(places(0, MQ, BANK), second)
-        nc.gpsimd.tensor_tensor(entry[0][:, BANK:], entry[0][:, BANK:], weight[0][:, BANK:], MULT)
-        nc.vector.tensor_copy(places(0, BANK, S), entry[0][:, BANK:])
+        pieces = [slice(lo, lo + MQ) for lo in range(0, BANK, MQ)]
+        for piece in pieces:
+            damping(exposure[0, 0], 0, 0, piece.start, piece.stop)
+        for piece in pieces:
+            nc.vector.tensor_tensor(damp[0][:, piece], signal[0, 0][:, piece], damp[0][:, piece], MULT)
+        for piece in pieces:
+            nc.vector.tensor_tensor(entry[0][:, piece], damp[0][:, piece], weight[0][:, piece], MULT)
+        for piece in pieces:
+            put(0, piece.start, piece.stop)
 
-        for t in range(1, PACK):
-            entry[t] = ring.tile([P, S], F32, name="entry", bufs=3)
-            for h in range(HALVES):
-                if (t, h) in later:
-                    exposure[t, h] = psum.tile([P, BANK], F32, name="exposure", tag="bank_b")
-                    signal[t, h] = psum.tile([P, BANK], F32, name="signal", tag="bank_a")
-                    for a in range(PASSES):
-                        exposure_pass(exposure[t, h], a, t, h)
-                    for a in range(PASSES):
-                        signal_pass(signal[t, h], a, t, h)
-                damping(exposure[t, h], t, h)
-                nc.scalar.copy(entry[t][:, cols(h)], signal[t, h][:])
-                nc.gpsimd.tensor_tensor(damp[t][:, cols(h)], damp[t][:, cols(h)], weight[t][:, cols(h)], MULT)
-                nc.gpsimd.tensor_tensor(entry[t][:, cols(h)], entry[t][:, cols(h)], damp[t][:, cols(h)], MULT)
+        for t, h in blocks[1:]:
+            if h == 0:
+                entry[t] = ring.tile([P, S], F32, name="entry", bufs=3)
+            number = HALVES * (1 + (t - 1) % 2) + h
+            if (t, h) not in opened:
+                exposure[t, h] = bank(number, [P, BANK])
+                for a in range(PASSES):
+                    exposure_pass(exposure[t, h], a, t, h)
+            damping(exposure[t, h], t, h)
+            if t > 0:
+                signal[t, h] = bank(number, [P, BANK])
+                for a in range(PASSES):
+                    signal_pass(signal[t, h], a, t, h)
+            nc.scalar.copy(entry[t][:, cols(h)], signal[t, h][:])
+            factor = weight[0][:, cols(0)] if t == 0 else damp[t][:, cols(h)]
+            nc.gpsimd.tensor_tensor(factor, damp[t][:, cols(h)], weight[t][:, cols(h)], MULT)
+            nc.gpsimd.tensor_tensor(entry[t][:, cols(h)], entry[t][:, cols(h)], factor, MULT)
 
-        def fetch(t, first_part, parts, fetched, gate, on_vector):
+        def fetch(t, first_part, parts, fetched, gate, engine):
             lo, hi = first_part * MQ, (first_part + parts) * MQ
             nc.vector.tensor_copy(fetched, page[t][:].indirect(idx3[:, lo // LIST_ROW : hi // LIST_ROW]))
             nc.scalar.activation(gate, fetched, ACT.Sigmoid, bias=bias_sb[:, t : t + 1])
             for u in range(parts):
                 slot = z[first_part + u][:, :, t]
-                if on_vector:
+                if engine == "scalar":
+                    nc.scalar.activation(slot, gate[:, cols(u, MQ)], ACT.Copy, scale=gain_sb[:, t : t + 1])
+                elif engine == "vector":
                     nc.vector.tensor_scalar(slot, gate[:, cols(u, MQ)], gain_sb[:, t : t + 1], None, MULT)
                 else:
-                    nc.scalar.activation(slot, gate[:, cols(u, MQ)], ACT.Copy, scale=gain_sb[:, t : t + 1])
+                    nc.gpsimd.tensor_scalar(slot, gate[:, cols(u, MQ)], gain_sb[:, t : t + 1], 0.0, MULT, ADD)
 
         def quantize_z(part):
             nc.vector.quantize_mx(
@@ -276,31 +286,32 @@ def tile_list_coupon_redemption_ratios_kernel(
             )
 
         for t in range(PACK):
-            if t > 0:
-                nc.vector.tensor_copy(places(t, 0, S), entry[t][:])
+            put(t, BANK if t == 0 else 0, S)
             gate = keep.tile([P, S], F32, name="scratch")
             if t + 1 < PACK:
                 parts = EARLY if t + 2 == PACK else M // MQ
-                fetch(t, 0, parts, weight[t][:, : parts * MQ], gate[:, : parts * MQ], False)
+                fetch(t, 0, parts, weight[t][:, : parts * MQ], gate[:, : parts * MQ], "scalar")
             else:
                 for part in range(EARLY):
-                    fetch(t, part, 1, damp[0][:, cols(part, MQ)], gate[:, cols(part, MQ)], True)
+                    fetch(t, part, 1, damp[0][:, cols(part, MQ)], gate[:, cols(part, MQ)], "vector")
                     quantize_z(part)
                 for part in range(EARLY, M // MQ):
                     late = keep.tile([P, 2, MQ], F32, name="late", tag="z", bufs=M // MQ, align_bytes=64)
                     for i in range(2):
-                        fetch(t - 1 + i, part, 1, late[:, i, :], late[:, i, :], True)
+                        fetch(t - 1 + i, part, 1, late[:, i, :], late[:, i, :], "gpsimd")
                     quantize_z(part)
 
         out_rows = out.rearrange("(c p) m -> p c m", p=P)
         pair = BANK // MQ
+        filled = 0
         for part in range(M // MQ):
             where = cols(part, MQ)
             staged = ring.tile([P, N // P, MQ], F32, name="staged", tag="wide", bufs=3, align_bytes=64)
             per_bank = 1 if part in (0, M // MQ - 1) else pair
             per_store = 1 if part == 0 else pair
             for i in range(N // P // per_bank):
-                scores = psum.tile([P, per_bank, MQ], F32, name="scores", tag="bank_b" if i % 2 else "bank_a")
+                scores = bank(filled % BANKS, [P, per_bank, MQ])
+                filled = filled + 1
                 for c in range(per_bank):
                     n_cols = cols(i * per_bank + c, P)
                     nc.tensor.matmul_mx(
@@ -313,7 +324,7 @@ def tile_list_coupon_redemption_ratios_kernel(
                         stop=True,
                     )
                 rows = slice(i * per_bank, (i + 1) * per_bank)
-                if part < EARLY or (i + part) % 2:
+                if part == 0 or (part == 1 and i == 2) or (part > 1 and i % 2 == 0):
                     nc.scalar.copy(staged[:, rows, :], scores[:])
                 else:
                     nc.vector.tensor_copy(staged[:, rows, :], scores[:])

@@ -58,11 +58,11 @@ def tile_list_coupon_redemption_ratios_kernel(
         tab_sc = held("tab_sc", [P, T], U8)
         picked = [held("picked%d" % a, [P, S], U32) for a in range(PASSES)]
         picked_sc_rows = held("picked_sc_rows", [P, S], U8)
-        picked_sc = held("picked_sc", [P, PASSES * S], U8)
+        sc_rows = held("sc_rows", [P, S + H], U8)
+        planes = held("planes", [P, PASSES * (S + H)], U8)
         w4_raw = held("w4_raw", [P, PASSES * H * 2], U8)
         w4 = held("w4", [P, PASSES * H * 2], U8)
-        w4_sc_raw = held("w4_sc_raw", [P, PASSES * H], U8)
-        w4_sc = held("w4_sc", [P, PASSES * H], U8)
+        w4_sc_rows = held("w4_sc_rows", [P, H], U8)
         w1_codes = [held("w1_codes%d" % a, [P, H], U32) for a in range(PASSES)]
         w1_sc = [held("w1_sc%d" % a, [P, H], U8) for a in range(PASSES)]
         w8 = held("w8", [P, N], I32)
@@ -82,8 +82,8 @@ def tile_list_coupon_redemption_ratios_kernel(
         nc.vector.memset(tab_sc[:].bitcast(I32), 0)
         nc.vector.memset(warm[:, 0:1], 1.0)
         nc.scalar.activation(warm[:, 1:2], warm[:, 0:1], ACT.Abs_reciprocal_sqrt)
-        nc.vector.memset(w4_sc_raw[:].bitcast(I32), 0)
-        nc.vector.memset(picked_sc[:].bitcast(I32), 0)
+        nc.vector.memset(w4_sc_rows[:].bitcast(I32), 0)
+        nc.vector.memset(planes[:].bitcast(I32), 0)
         nc.vector.memset(w8_sc[:].bitcast(I32), 0)
         make_identity(nc, ident[:])
 
@@ -104,16 +104,14 @@ def tile_list_coupon_redemption_ratios_kernel(
             tab_sc[0 : 2 * PASSES * 16 : 2, :].bitcast(I32), tab_scales.bitcast(I32).rearrange("a q t -> q a t")
         )
         nc.sync.dma_start(idx[:], offs)
+        nc.sync.dma_start(
+            w4_sc_rows[0 : 2 * PASSES * 16 : 2, :].bitcast(I32), w4_scales.bitcast(I32).rearrange("a q c -> q a c")
+        )
         nc.sync.dma_start(wgs_rows[:], wgs)
         nc.sync.dma_start(
             w4_raw[:].bitcast(I32).rearrange("p (a c) -> p a c", a=PASSES), w4_words.bitcast(I32).rearrange("a p c -> p a c")
         )
         load_tab(0)
-        for q in range(QUADS):
-            nc.sync.dma_start(
-                w4_sc_raw[32 * q : 32 * q + 4, :].bitcast(I32).rearrange("p (a c) -> p a c", a=PASSES),
-                w4_scales.bitcast(I32)[:, 4 * q : 4 * q + 4, :].rearrange("a r c -> r a c"),
-            )
         load_w1(1)
         load_tab(1)
         load_tab(2)
@@ -144,19 +142,22 @@ def tile_list_coupon_redemption_ratios_kernel(
 
         quantize_w1(0, 0, PACK, nc.vector.tensor_copy)
         nc.vector.tensor_copy(picked_sc_rows[:], tab_sc[:].indirect(idx[:]))
+        nc.vector.tensor_copy(sc_rows[:, :S].bitcast(I32), picked_sc_rows[:].bitcast(I32))
+        nc.vector.tensor_copy(
+            sc_rows[:, S:].rearrange("p (t m) -> p t m", t=PACK), w4_sc_rows[:].rearrange("p (m t) -> p t m", t=PACK)
+        )
         for q in range(QUADS):
-            nc.scalar.dma_start(
-                picked_sc[32 * q : 32 * q + 4, :].bitcast(I32).rearrange("p (a c) -> p a c", a=PASSES),
-                picked_sc_rows[24 * q : 24 * q + 24 : 2, :].bitcast(I32),
+            nc.gpsimd.dma_start(
+                planes[32 * q : 32 * q + 4, :].bitcast(I32).rearrange("p (a c) -> p a c", a=PASSES),
+                sc_rows[24 * q : 24 * q + 24 : 2, :].bitcast(I32),
             )
         nc.vector.tensor_copy(
             w4[:].bitcast(U16).rearrange("p (a t m) -> p a t m", a=PASSES, t=PACK),
             w4_raw[:].bitcast(U16).rearrange("p (a m t) -> p a t m", a=PASSES, t=PACK),
         )
-        nc.vector.tensor_copy(
-            w4_sc[:].rearrange("p (a t m) -> p a t m", a=PASSES, t=PACK),
-            w4_sc_raw[:].rearrange("p (a m t) -> p a t m", a=PASSES, t=PACK),
-        )
+
+        def plane(a, first, width):
+            return planes[:, a * (S + H) + first : a * (S + H) + first + width]
 
         for h in range(HALVES):
             turned = bank(h, [P, PACK, P])
@@ -179,9 +180,9 @@ def tile_list_coupon_redemption_ratios_kernel(
             nc.tensor.matmul_mx(
                 out=acc[:],
                 lhsT=w4[:, 2 * c0 : 2 * (c0 + P)].bitcast(FP4X4),
-                lhsT_scale=w4_sc[:, c0 : c0 + P],
+                lhsT_scale=plane(a, S + t * P, P),
                 rhs=picked[a][:, cols(h)].bitcast(FP8X4),
-                rhs_scale=picked_sc[:, a * S + h * BANK : a * S + (h + 1) * BANK],
+                rhs_scale=plane(a, h * BANK, BANK),
                 start=(a == 0),
                 stop=(a == PASSES - 1),
             )
@@ -192,7 +193,7 @@ def tile_list_coupon_redemption_ratios_kernel(
                 lhsT=w1_codes[a][:, cols(t, P)].bitcast(FP8X4),
                 lhsT_scale=w1_sc[a][:, cols(t, P)],
                 rhs=picked[a][:, cols(h)].bitcast(FP8X4),
-                rhs_scale=picked_sc[:, a * S + h * BANK : a * S + (h + 1) * BANK],
+                rhs_scale=plane(a, h * BANK, BANK),
                 start=(a == 0),
                 stop=(a == PASSES - 1),
             )

@@ -247,8 +247,7 @@ def tile_list_coupon_redemption_ratios_kernel(
             nc.vector.tensor_tensor(damp[0][:, piece], signal[0, 0][:, piece], damp[0][:, piece], MULT)
         for piece in pieces:
             nc.vector.tensor_tensor(entry[0][:, piece], damp[0][:, piece], weight[0][:, piece], MULT)
-        for piece in pieces:
-            put(0, piece.start, piece.stop)
+        put(0, 0, BANK)
 
         for t, h in blocks[1:]:
             if h == 0:
@@ -288,11 +287,15 @@ def tile_list_coupon_redemption_ratios_kernel(
 
         for t in range(PACK):
             put(t, BANK if t == 0 else 0, S)
-            gate = keep.tile([P, S], F32, name="scratch")
-            if t + 1 < PACK:
-                parts = EARLY if t + 2 == PACK else M // MQ
-                fetch(t, 0, parts, weight[t][:, : parts * MQ], gate[:, : parts * MQ], "scalar")
-            else:
+            if t != 1:
+                gate = keep.tile([P, S], F32, name="scratch")
+            if t == 0:
+                fetch(0, 0, M // MQ, weight[0][:], gate[:], "scalar")
+            elif t == 2:
+                fetch(1, 0, M // MQ, entry[2][:], gate[:], "scalar")
+                gate = keep.tile([P, S], F32, name="scratch")
+                fetch(2, 0, EARLY, weight[2][:, : EARLY * MQ], gate[:, : EARLY * MQ], "scalar")
+            elif t == 3:
                 for part in range(EARLY):
                     fetch(t, part, 1, damp[0][:, cols(part, MQ)], gate[:, cols(part, MQ)], "vector")
                     quantize_z(part)

@@ -134,8 +134,8 @@ def tile_list_coupon_redemption_ratios_kernel(
         def quantize_w1(a, t0, t1, cast):
             grouped = ring.tile([P, (t1 - t0) * P * PACK], BF16, name="w1_grouped", align_bytes=64)
             cast(
-                grouped[:].rearrange("p (t m j) -> p m t j", t=t1 - t0, j=PACK),
-                w1_raw[a][:].rearrange("p j (m t) -> p m t j", t=PACK)[:, :, t0:t1, :],
+                grouped[:].rearrange("p (t m j) -> p m j t", t=t1 - t0, j=PACK),
+                w1_raw[a][:].rearrange("p j (m t) -> p m j t", t=PACK)[:, :, :, t0:t1],
             )
             where = slice(t0 * P, t1 * P)
             nc.vector.quantize_mx(out=w1_codes[a][:, where].bitcast(FP8X4), scales=w1_sc[a][:, where], in_=grouped[:])

@@ -131,16 +131,19 @@ def tile_list_coupon_redemption_ratios_kernel(
         def gather_words(a, picks, where):
             nc.vector.tensor_copy(picked[a][:, where], tab[a][:].bitcast(U32).indirect(picks))
 
-        def quantize_w1(a, t0, t1, cast):
+        def round_w1(a, t0, t1):
             grouped = ring.tile([P, (t1 - t0) * P * PACK], BF16, name="w1_grouped", align_bytes=64)
-            cast(
+            nc.vector.tensor_copy(
                 grouped[:].rearrange("p (t m j) -> p m j t", t=t1 - t0, j=PACK),
                 w1_raw[a][:].rearrange("p j (m t) -> p m j t", t=PACK)[:, :, :, t0:t1],
             )
+            return grouped
+
+        def quantize_w1(a, t0, t1, grouped):
             where = slice(t0 * P, t1 * P)
             nc.vector.quantize_mx(out=w1_codes[a][:, where].bitcast(FP8X4), scales=w1_sc[a][:, where], in_=grouped[:])
 
-        quantize_w1(0, 0, PACK, nc.vector.tensor_copy)
+        quantize_w1(0, 0, PACK, round_w1(0, 0, PACK))
         nc.vector.tensor_copy(picked_sc_rows[:], tab_sc[:].indirect(idx[:]))
         nc.vector.tensor_copy(sc_rows[:, :S].bitcast(I32), picked_sc_rows[:].bitcast(I32))
         nc.vector.tensor_copy(
@@ -200,14 +203,19 @@ def tile_list_coupon_redemption_ratios_kernel(
 
         scratch = {}
 
-        def damping(acc, t, h, lo=0, hi=BANK):
-            if h == 0 and lo == 0:
+        def damping(acc, t, h):
+            if h == 0:
                 scratch[t] = keep.tile([P, S], F32, name="scratch")
-            where = slice(h * BANK + lo, h * BANK + hi)
-            part = scratch[t][:, where]
-            nc.scalar.activation(part, acc[:, lo:hi], ACT.Square)
-            nc.scalar.activation(part, part, ACT.Abs_reciprocal_sqrt, bias=1.0)
-            nc.scalar.activation(damp[t][:, where], part, ACT.Square)
+            width = MQ if t == 0 else BANK
+            work = scratch[t][:, cols(0 if t == 0 else h)]
+            result = work if (t, h) == (0, 1) else damp[t][:, cols(h)]
+            spans = [cols(i, width) for i in range(BANK // width)]
+            for span in spans:
+                nc.scalar.activation(work[:, span], acc[:, span], ACT.Square)
+            for span in spans:
+                nc.scalar.activation(work[:, span], work[:, span], ACT.Abs_reciprocal_sqrt, bias=1.0)
+            for span in spans:
+                nc.scalar.activation(result[:, span], work[:, span], ACT.Square)
 
         blocks = [(t, h) for t in range(PACK) for h in range(HALVES)]
         opened = blocks[: 2 * HALVES]
@@ -215,7 +223,7 @@ def tile_list_coupon_redemption_ratios_kernel(
         signal = {(0, h): bank(2 * HALVES + h, [P, BANK]) for h in range(HALVES)}
 
         gather_words(0, idx[:], slice(0, S))
-        quantize_w1(1, 0, PACK, nc.vector.tensor_copy)
+        quantize_w1(1, 0, PACK, round_w1(1, 0, PACK))
         gather_words(1, idx[:], slice(0, S))
         last = PASSES - 1
         for a in range(last):
@@ -227,8 +235,9 @@ def tile_list_coupon_redemption_ratios_kernel(
             gather_words(last, idx[:, entries(h)], cols(h))
         for h in range(HALVES):
             exposure_pass(exposure[0, h], last, 0, h)
-        quantize_w1(last, 0, 2, nc.vector.tensor_copy)
-        quantize_w1(last, 2, PACK, nc.vector.tensor_copy)
+        rounded = [round_w1(last, t0, t0 + 2) for t0 in (0, 2)]
+        for t0 in (0, 2):
+            quantize_w1(last, t0, t0 + 2, rounded[t0 // 2])
         for h in range(HALVES):
             signal_pass(signal[0, h], last, 0, h)
         for t, h in opened[HALVES:]:
@@ -241,12 +250,11 @@ def tile_list_coupon_redemption_ratios_kernel(
 
         entry[0] = ring.tile([P, S], F32, name="entry", bufs=3)
         pieces = [slice(lo, lo + MQ) for lo in range(0, BANK, MQ)]
+        damping(exposure[0, 0], 0, 0)
+        first_factor = rounded[0][:].bitcast(F32)
         for piece in pieces:
-            damping(exposure[0, 0], 0, 0, piece.start, piece.stop)
-        for piece in pieces:
-            nc.vector.tensor_tensor(damp[0][:, piece], signal[0, 0][:, piece], damp[0][:, piece], MULT)
-        for piece in pieces:
-            nc.vector.tensor_tensor(entry[0][:, piece], damp[0][:, piece], weight[0][:, piece], MULT)
+            nc.vector.tensor_tensor(first_factor[:, piece], damp[0][:, piece], weight[0][:, piece], MULT)
+        nc.vector.tensor_tensor(entry[0][:, cols(0)], signal[0, 0][:], first_factor, MULT)
         put(0, 0, BANK)
 
         for t, h in blocks[1:]:
@@ -259,13 +267,17 @@ def tile_list_coupon_redemption_ratios_kernel(
                     exposure_pass(exposure[t, h], a, t, h)
             damping(exposure[t, h], t, h)
             if t > 0:
-                signal[t, h] = bank(number, [P, BANK])
+                signal[t, h] = bank(BANKS - HALVES + h if t == 1 else number, [P, BANK])
                 for a in range(PASSES):
                     signal_pass(signal[t, h], a, t, h)
             nc.scalar.copy(entry[t][:, cols(h)], signal[t, h][:])
-            factor = weight[0][:, cols(0)] if t == 0 else damp[t][:, cols(h)]
-            nc.gpsimd.tensor_tensor(factor, damp[t][:, cols(h)], weight[t][:, cols(h)], MULT)
-            nc.gpsimd.tensor_tensor(entry[t][:, cols(h)], entry[t][:, cols(h)], factor, MULT)
+            values = entry[t][:, cols(h)]
+            if t == 0:
+                nc.gpsimd.tensor_tensor(weight[0][:, cols(0)], scratch[0][:, cols(0)], weight[0][:, cols(h)], MULT)
+                nc.gpsimd.tensor_tensor(values, values, weight[0][:, cols(0)], MULT)
+            else:
+                nc.gpsimd.tensor_tensor(values, values, weight[t][:, cols(h)], MULT)
+                nc.gpsimd.tensor_tensor(values, values, damp[t][:, cols(h)], MULT)
 
         def fetch(t, first_part, parts, fetched, gate, engine):
             lo, hi = first_part * MQ, (first_part + parts) * MQ

@@ -314,7 +314,7 @@ def tile_list_coupon_redemption_ratios_kernel(
                 for part in range(EARLY, M // MQ):
                     late = keep.tile([P, 2, MQ], F32, name="late", tag="z", bufs=M // MQ, align_bytes=64)
                     for i in range(2):
-                        fetch(t - 1 + i, part, 1, late[:, i, :], late[:, i, :], "gpsimd")
+                        fetch(t - 1 + i, part, 1, late[:, i, :], late[:, i, :], "gpsimd" if part == EARLY else "vector")
                     quantize_z(part)
 
         out_rows = out.rearrange("(c p) m -> p c m", p=P)

from contextlib import ExitStack

import concourse.mybir as mybir
from concourse.masks import make_identity

K, T, S, H, T2, M, N = 1536, 4096, 1024, 512, 2048, 1024, 768
FLOPS = 2 * 2 * K * H * S + 2 * H * N * M

F32 = mybir.dt.float32
BF16 = mybir.dt.bfloat16
I32 = mybir.dt.int32
U32 = mybir.dt.uint32
U16 = mybir.dt.uint16
U8 = mybir.dt.uint8
FP8X4 = mybir.dt.float8_e4m3fn_x4
FP4X4 = mybir.dt.float4_e2m1fn_x4
ACT = mybir.ActivationFunctionType
MULT = mybir.AluOpType.mult
ADD = mybir.AluOpType.add

P = 128
PACK = 4
PASSES = K // (P * PACK)
QUADS = 4
BANK = 512
HALVES = S // BANK
MQ = 256
LIST_ROW = 16
BANKS = 8
EARLY = 2


def tile_list_coupon_redemption_ratios_kernel(
    tc, tab_words, tab_scales, offs, w1, w4_words, w4_scales, page0, wgs, offs2, offs3, bias, gain, w8_words, w8_scales, out
):
    nc = tc.nc
    with ExitStack() as ctx:
        keep = ctx.enter_context(tc.tile_pool(name="keep", bufs=1))
        ring = ctx.enter_context(tc.tile_pool(name="ring", bufs=2))
        psum = ctx.enter_context(tc.psum_pool(name="psum", bufs=1))

        def held(name, shape, dtype):
            return keep.tile(shape, dtype, name=name, align_bytes=64)

        def bank(number, shape):
            return psum.tile(shape, F32, name="bank", tag="bank%d" % number)

        def cols(h, width=BANK):
            return slice(h * width, (h + 1) * width)

        def entries(h, width=BANK):
            return slice(h * width // LIST_ROW, (h + 1) * width // LIST_ROW)

        idx = held("idx", [P, S // LIST_ROW], U16)
        idx2 = held("idx2", [P, S // LIST_ROW], U16)
        idx3 = held("idx3", [P, M // LIST_ROW], U16)
        tab = [held("tab%d" % a, [P, T], I32) for a in range(PASSES)]
        tab_sc = held("tab_sc", [P, T], U8)
        picked = [held("picked%d" % a, [P, S], U32) for a in range(PASSES)]
        picked_sc_rows = held("picked_sc_rows", [P, S], U8)
        sc_rows = held("sc_rows", [P, S + H], U8)
        planes = held("planes", [P, PASSES * (S + H)], U8)
        w4_raw = held("w4_raw", [P, PASSES * H * 2], U8)
        w4 = held("w4", [P, PASSES * H * 2], U8)
        w4_sc_rows = held("w4_sc_rows", [P, H], U8)
        w1_codes = [held("w1_codes%d" % a, [P, H], U32) for a in range(PASSES)]
        w1_sc = [held("w1_sc%d" % a, [P, H], U8) for a in range(PASSES)]
        w8 = held("w8", [P, N], I32)
        w8_sc = held("w8_sc", [P, N], U8)
        page = [held("page%d" % t, [P, T2], F32) for t in range(PACK)]
        wgs_rows = held("wgs_rows", [P, S], F32)
        weight = [held("weight%d" % t, [P, S], F32) for t in range(PACK)]
        damp = [held("damp%d" % t, [P, S], F32) for t in range(PACK)]
        bias_sb = held("bias_sb", [P, PACK], F32)
        gain_sb = held("gain_sb", [P, PACK], F32)
        z = [keep.tile([P, MQ, PACK], BF16, name="z", tag="z", bufs=M // MQ, align_bytes=64) for u in range(M // MQ)]
        z_codes = [held("z_codes%d" % u, [P, MQ], U32) for u in range(M // MQ)]
        z_sc = [held("z_sc%d" % u, [P, MQ], U8) for u in range(M // MQ)]
        ident = held("ident", [P, P], F32)
        warm = held("warm", [P, 2], F32)

        nc.vector.memset(tab_sc[:].bitcast(I32), 0)
        nc.vector.memset(warm[:, 0:1], 1.0)
        nc.scalar.activation(warm[:, 1:2], warm[:, 0:1], ACT.Abs_reciprocal_sqrt)
        nc.vector.memset(w4_sc_rows[:].bitcast(I32), 0)
        nc.vector.memset(planes[:].bitcast(I32), 0)
        nc.vector.memset(w8_sc[:].bitcast(I32), 0)
        make_identity(nc, ident[:])

        def load_tab(a):
            nc.sync.dma_start(tab[a][:], tab_words[a].rearrange("p t i -> p (t i)").bitcast(I32))

        w1_raw = {}

        def load_w1(a):
            w1_raw[a] = ring.tile([P, PACK, H], F32, name="w1_raw", tag="wide", bufs=3, align_bytes=64)
            nc.sync.dma_start(w1_raw[a][:], w1[a * P * PACK : (a + 1) * P * PACK, :].rearrange("(p j) r -> p j r", j=PACK))

        def load_page(t):
            nc.sync.dma_start(page[t][:], page0.rearrange("(p t) c -> p t c", t=PACK)[:, t, :])

        load_w1(0)
        nc.sync.dma_start(
            tab_sc[0 : 2 * PASSES * 16 : 2, :].bitcast(I32), tab_scales.bitcast(I32).rearrange("a q t -> q a t")
        )
        nc.sync.dma_start(idx[:], offs)
        nc.sync.dma_start(
            w4_sc_rows[0 : 2 * PASSES * 16 : 2, :].bitcast(I32), w4_scales.bitcast(I32).rearrange("a q c -> q a c")
        )
        nc.sync.dma_start(wgs_rows[:], wgs)
        nc.sync.dma_start(
            w4_raw[:].bitcast(I32).rearrange("p (a c) -> p a c", a=PASSES), w4_words.bitcast(I32).rearrange("a p c -> p a c")
        )
        load_tab(0)
        load_w1(1)
        load_tab(1)
        load_tab(2)
        load_w1(2)
        nc.sync.dma_start(idx2[:], offs2)
        load_page(0)
        nc.sync.dma_start(idx3[:], offs3)
        load_page(1)
        nc.sync.dma_start(bias_sb[:], bias.rearrange("(p t) -> p t", t=PACK))
        nc.sync.dma_start(gain_sb[:], gain.rearrange("(p t) -> p t", t=PACK))
        load_page(2)
        load_page(3)
        nc.sync.dma_start(w8[:], w8_words[0].rearrange("p c i -> p (c i)").bitcast(I32))
        for q in range(QUADS):
            nc.sync.dma_start(w8_sc[32 * q : 32 * q + 4, :].bitcast(I32), w8_scales.bitcast(I32)[0, 4 * q : 4 * q + 4, :])

        def gather_words(a, picks, where):
            nc.vector.tensor_copy(picked[a][:, where], tab[a][:].bitcast(U32).indirect(picks))

        def round_w1(a, t0, t1):
            grouped = ring.tile([P, (t1 - t0) * P * PACK], BF16, name="w1_grouped", align_bytes=64)
            nc.vector.tensor_copy(
                grouped[:].rearrange("p (t m j) -> p m j t", t=t1 - t0, j=PACK),
                w1_raw[a][:].rearrange("p j (m t) -> p m j t", t=PACK)[:, :, :, t0:t1],
            )
            return grouped

        def quantize_w1(a, t0, t1, grouped):
            where = slice(t0 * P, t1 * P)
            nc.vector.quantize_mx(out=w1_codes[a][:, where].bitcast(FP8X4), scales=w1_sc[a][:, where], in_=grouped[:])

        quantize_w1(0, 0, PACK, round_w1(0, 0, PACK))
        nc.vector.tensor_copy(picked_sc_rows[:], tab_sc[:].indirect(idx[:]))
        nc.vector.tensor_copy(sc_rows[:, :S].bitcast(I32), picked_sc_rows[:].bitcast(I32))
        nc.vector.tensor_copy(
            sc_rows[:, S:].rearrange("p (t m) -> p t m", t=PACK), w4_sc_rows[:].rearrange("p (m t) -> p t m", t=PACK)
        )
        for q in range(QUADS):
            nc.gpsimd.dma_start(
                planes[32 * q : 32 * q + 4, :].bitcast(I32).rearrange("p (a c) -> p a c", a=PASSES),
                sc_rows[24 * q : 24 * q + 24 : 2, :].bitcast(I32),
            )
        nc.vector.tensor_copy(
            w4[:].bitcast(U16).rearrange("p (a t m) -> p a t m", a=PASSES, t=PACK),
            w4_raw[:].bitcast(U16).rearrange("p (a m t) -> p a t m", a=PASSES, t=PACK),
        )

        def plane(a, first, width):
            return planes[:, a * (S + H) + first : a * (S + H) + first + width]

        for h in range(HALVES):
            turned = bank(h, [P, PACK, P])
            for i in range(PACK):
                nc.tensor.transpose(turned[:, i, :], wgs_rows[:, cols(h * PACK + i, P)], ident[:])
            spread = ring.tile([P, PACK, PACK, QUADS, 32], F32, name="spread")
            for i in range(PACK):
                nc.scalar.copy(
                    spread[:, i],
                    turned[:, i, :].rearrange("j (q t) -> j t q", t=PACK).unsqueeze(2).to_broadcast([P, PACK, QUADS, 32]),
                )
            for t in range(PACK):
                back = bank(PACK + t, [P, PACK, P])
                for i in range(PACK):
                    nc.tensor.transpose(back[:, i, :], spread[:, i, t].rearrange("j u q -> j (u q)"), ident[:])
                nc.scalar.copy(weight[t][:, cols(h)], back[:].rearrange("p i j -> p (i j)"))

        def exposure_pass(acc, a, t, h):
            c0 = a * H + t * P
            nc.tensor.matmul_mx(
                out=acc[:],
                lhsT=w4[:, 2 * c0 : 2 * (c0 + P)].bitcast(FP4X4),
                lhsT_scale=plane(a, S + t * P, P),
                rhs=picked[a][:, cols(h)].bitcast(FP8X4),
                rhs_scale=plane(a, h * BANK, BANK),
                start=(a == 0),
                stop=(a == PASSES - 1),
            )

        def signal_pass(acc, a, t, h):
            nc.tensor.matmul_mx(
                out=acc[:],
                lhsT=w1_codes[a][:, cols(t, P)].bitcast(FP8X4),
                lhsT_scale=w1_sc[a][:, cols(t, P)],
                rhs=picked[a][:, cols(h)].bitcast(FP8X4),
                rhs_scale=plane(a, h * BANK, BANK),
                start=(a == 0),
                stop=(a == PASSES - 1),
            )

        scratch = {}

        def damping(acc, t, h):
            if h == 0:
                scratch[t] = keep.tile([P, S], F32, name="scratch")
            width = MQ if t == 0 else BANK
            work = scratch[t][:, cols(0 if t == 0 else h)]
            result = work if (t, h) == (0, 1) else damp[t][:, cols(h)]
            spans = [cols(i, width) for i in range(BANK // width)]
            for span in spans:
                nc.scalar.activation(work[:, span], acc[:, span], ACT.Square)
            for span in spans:
                nc.scalar.activation(work[:, span], work[:, span], ACT.Abs_reciprocal_sqrt, bias=1.0)
            for span in spans:
                nc.scalar.activation(result[:, span], work[:, span], ACT.Square)

        blocks = [(t, h) for t in range(PACK) for h in range(HALVES)]
        opened = blocks[: 2 * HALVES]
        exposure = {(t, h): bank(HALVES * t + h, [P, BANK]) for t, h in opened}
        signal = {(0, h): bank(2 * HALVES + h, [P, BANK]) for h in range(HALVES)}

        gather_words(0, idx[:], slice(0, S))
        quantize_w1(1, 0, PACK, round_w1(1, 0, PACK))
        gather_words(1, idx[:], slice(0, S))
        last = PASSES - 1
        for a in range(last):
            for t, h in opened:
                exposure_pass(exposure[t, h], a, t, h)
            for h in range(HALVES):
                signal_pass(signal[0, h], a, 0, h)
        for h in range(HALVES):
            gather_words(last, idx[:, entries(h)], cols(h))
        for h in range(HALVES):
            exposure_pass(exposure[0, h], last, 0, h)
        rounded = [round_w1(last, t0, t0 + 2) for t0 in (0, 2)]
        for t0 in (0, 2):
            quantize_w1(last, t0, t0 + 2, rounded[t0 // 2])
        for h in range(HALVES):
            signal_pass(signal[0, h], last, 0, h)
        for t, h in opened[HALVES:]:
            exposure_pass(exposure[t, h], last, t, h)

        entry = {}

        def put(t, lo, hi):
            nc.vector.tensor_copy(page[t][:].indirect(idx2[:, lo // LIST_ROW : hi // LIST_ROW]), entry[t][:, lo:hi])

        entry[0] = ring.tile([P, S], F32, name="entry", bufs=3)
        pieces = [slice(lo, lo + MQ) for lo in range(0, BANK, MQ)]
        damping(exposure[0, 0], 0, 0)
        first_factor = rounded[0][:].bitcast(F32)
        for piece in pieces:
            nc.vector.tensor_tensor(first_factor[:, piece], damp[0][:, piece], weight[0][:, piece], MULT)
        nc.vector.tensor_tensor(entry[0][:, cols(0)], signal[0, 0][:], first_factor, MULT)
        put(0, 0, BANK)

        for t, h in blocks[1:]:
            if h == 0:
                entry[t] = ring.tile([P, S], F32, name="entry", bufs=3)
            number = HALVES * (1 + (t - 1) % 2) + h
            if (t, h) not in opened:
                exposure[t, h] = bank(number, [P, BANK])
                for a in range(PASSES):
                    exposure_pass(exposure[t, h], a, t, h)
            damping(exposure[t, h], t, h)
            if t > 0:
                signal[t, h] = bank(BANKS - HALVES + h if t == 1 else number, [P, BANK])
                for a in range(PASSES):
                    signal_pass(signal[t, h], a, t, h)
            nc.scalar.copy(entry[t][:, cols(h)], signal[t, h][:])
            values = entry[t][:, cols(h)]
            if t == 0:
                nc.gpsimd.tensor_tensor(weight[0][:, cols(0)], scratch[0][:, cols(0)], weight[0][:, cols(h)], MULT)
                nc.gpsimd.tensor_tensor(values, values, weight[0][:, cols(0)], MULT)
            else:
                nc.gpsimd.tensor_tensor(values, values, weight[t][:, cols(h)], MULT)
                nc.gpsimd.tensor_tensor(values, values, damp[t][:, cols(h)], MULT)

        def fetch(t, first_part, parts, fetched, gate, engine):
            lo, hi = first_part * MQ, (first_part + parts) * MQ
            nc.vector.tensor_copy(fetched, page[t][:].indirect(idx3[:, lo // LIST_ROW : hi // LIST_ROW]))
            nc.scalar.activation(gate, fetched, ACT.Sigmoid, bias=bias_sb[:, t : t + 1])
            for u in range(parts):
                slot = z[first_part + u][:, :, t]
                if engine == "scalar":
                    nc.scalar.activation(slot, gate[:, cols(u, MQ)], ACT.Copy, scale=gain_sb[:, t : t + 1])
                elif engine == "vector":
                    nc.vector.tensor_scalar(slot, gate[:, cols(u, MQ)], gain_sb[:, t : t + 1], None, MULT)
                else:
                    nc.gpsimd.tensor_scalar(slot, gate[:, cols(u, MQ)], gain_sb[:, t : t + 1], 0.0, MULT, ADD)

        def quantize_z(part):
            nc.vector.quantize_mx(
                out=z_codes[part][:].bitcast(FP8X4), scales=z_sc[part][:], in_=z[part][:].rearrange("p m t -> p (m t)")
            )

        for t in range(PACK):
            put(t, BANK if t == 0 else 0, S)
            if t != 1:
                gate = keep.tile([P, S], F32, name="scratch")
            if t == 0:
                fetch(0, 0, M // MQ, weight[0][:], gate[:], "scalar")
            elif t == 2:
                fetch(1, 0, M // MQ, entry[2][:], gate[:], "scalar")
                gate = keep.tile([P, S], F32, name="scratch")
                fetch(2, 0, EARLY, weight[2][:, : EARLY * MQ], gate[:, : EARLY * MQ], "scalar")
            elif t == 3:
                for part in range(EARLY):
                    fetch(t, part, 1, damp[0][:, cols(part, MQ)], gate[:, cols(part, MQ)], "vector")
                    quantize_z(part)
                for part in range(EARLY, M // MQ):
                    late = keep.tile([P, 2, MQ], F32, name="late", tag="z", bufs=M // MQ, align_bytes=64)
                    for i in range(2):
                        fetch(t - 1 + i, part, 1, late[:, i, :], late[:, i, :], "gpsimd" if part == EARLY else "vector")
                    quantize_z(part)

        out_rows = out.rearrange("(c p) m -> p c m", p=P)
        pair = BANK // MQ
        filled = 0
        for part in range(M // MQ):
            where = cols(part, MQ)
            staged = ring.tile([P, N // P, MQ], F32, name="staged", tag="wide", bufs=3, align_bytes=64)
            per_bank = 1 if part in (0, M // MQ - 1) else pair
            per_store = 1 if part == 0 else pair
            for i in range(N // P // per_bank):
                scores = bank(filled % BANKS, [P, per_bank, MQ])
                filled = filled + 1
                for c in range(per_bank):
                    n_cols = cols(i * per_bank + c, P)
                    nc.tensor.matmul_mx(
                        out=scores[:, c, :],
                        lhsT=w8[:, n_cols].bitcast(FP8X4),
                        lhsT_scale=w8_sc[:, n_cols],
                        rhs=z_codes[part][:].bitcast(FP8X4),
                        rhs_scale=z_sc[part][:],
                        start=True,
                        stop=True,
                    )
                rows = slice(i * per_bank, (i + 1) * per_bank)
                if part == 0 or (part == 1 and i == 2) or (part > 1 and i % 2 == 0):
                    nc.scalar.copy(staged[:, rows, :], scores[:])
                else:
                    nc.vector.tensor_copy(staged[:, rows, :], scores[:])
                if rows.stop % per_store == 0:
                    both = slice(rows.stop - per_store, rows.stop)
                    nc.sync.dma_start(out_rows[:, both, where], staged[:, both, :])
